import numpy as np, ml_dtypes
CORES = [48,51,52,55]
N = 4
BF = ml_dtypes.bfloat16
def gentries(a):
    return np.ascontiguousarray(a.reshape(8, 16, -1).transpose(0, 2, 1)).reshape(8, -1)
def gtable(e):
    e = np.asarray(e); return np.ascontiguousarray(e.reshape(8, -1, 16).transpose(0, 2, 1)).reshape(128, -1).astype(np.int32)
W, K, L, T = 4608, 1024, 1, 3
TOP, NEG, EMPTY = 255, 9, 16
def parts(rng):
    j = rng.integers(0, W, (N, 8, 16, W), dtype=np.int32)
    x = rng.integers(0, 16, (N, 8, N, L, K)); x = np.where(rng.random(x.shape) < 0.125, EMPTY, x)
    return j, x, rng.integers(0, 16, (N, 8, K)), rng.integers(0, W, (N, 8, T, K))
def coef(rng, drift):
    c = drift + 50.0 * rng.standard_normal((N, 8, 1, W), dtype=np.float32) + 40.0 * rng.standard_normal((N, 8, 16, W), dtype=np.float32)
    return np.minimum(np.maximum(np.rint(c), -128), 127)
def pack(j, c, x, y, a):
    return {"jm": np.ascontiguousarray(j.reshape(N, 128, W)).astype(np.int32), "cf": (np.ascontiguousarray(c.reshape(N, 128, W)).astype(np.float32) + 0.0).astype(BF),
            "lt": np.ascontiguousarray(x.reshape(N, 8, N * L * K)).astype(np.float32).astype(BF), "y0": np.ascontiguousarray(y).astype(np.float32).astype(BF),
            "st": np.stack([gtable(q.reshape(8, T * K)) for q in a])}
def setup_inputs(rng):
    j, x, y, a = parts(rng)
    return pack(j, coef(rng, rng.choice(np.array([5.0, 15.0, 30.0, 45.0]), (N, 8, 1, 1))), x, y, a)
def setup_inputs_ties(rng):
    j, x, y, a = parts(rng); n = rng.choice(np.array([4, 6, 7, 8, 9]), (N, 8, 1, W))
    o = np.argsort(rng.random((N, 8, 16, W)), axis=2); c = np.where(o < n, -1, (rng.random(o.shape) < 0.8).astype(np.int64))
    p = rng.permutation(16)[:, None]
    c[:, 0] = np.where(p < 8, -1, 1); c[:, 1] = np.where(p < 9, -1, 1); c[:, 2] = np.where(p < 8, -1, 0)
    return pack(j, c, x, y, a)
def setup_inputs_clip(rng):
    j, x, y, a = parts(rng); s = np.where(rng.random((N, 8, 1, W)) < 0.75, 1, -1)
    c = s * rng.integers(100, 128, (N, 8, 16, W)); c = np.where(rng.random(c.shape) < 0.1, -c, c)
    c[:, 1::2, :5] = -np.abs(c[:, 1::2, :5]) - 1
    r = int(rng.integers(0, N)); x[:, 6, r] = rng.integers(0, 16, (N, L, K)); e = 127 // L
    for d in range(N):
        q = (r + d) % N; c[q, 6] = 1; c[q, 6, 1:8] = -1
        c[q, 6, 8] = -1 if d == 3 else 0
        c[q, 6, 0] = (-128, e, e, 255 - 2 * L * e)[d] if d < 4 else 0
    return pack(j, c, x, y, a)
def setup_inputs_gaps(rng):
    j, x, y, a = parts(rng); x = np.where(rng.random(x.shape) < 0.5, EMPTY, x)
    x[:, 0] = EMPTY; x[:, 1:4] = rng.integers(0, 16, (N, 3, N, L, K))
    for q in range(N):
        for s in range(N):
            if q != s: x[q, 2, s] = EMPTY
            if q != (s - 1) % N: x[q, 3, s] = EMPTY
    c = coef(rng, 20.0); r = int(rng.integers(0, N))
    c[r, 0] = -rng.integers(1, 129, (16, W)); c[r, 1] = -128; c[r, 1, 8:] += (rng.random(W) < 0.5).astype(np.float32)
    x[r, 1, r, 1:] = EMPTY
    return pack(j, c, x, y, a)
def setup_inputs_alike(rng):
    j, x, y, a = parts(rng)
    j[:, ::2] = rng.choice(np.array([0, W - 1, W // 2, 5], np.int32), (N, 4, 16, W)); j[:, 1] = np.arange(W)
    j[:, 6] = rng.integers(0, W, (N, 1, 1))
    x[:, 3] = rng.integers(0, 16, (N, 1, 1, 1)); y[:, 3] = rng.integers(0, 16, (N, 1))
    a[:, 2] = rng.integers(0, W, (N, 1, 1)); a[:, 5] = rng.choice(np.array([0, W - 1]), (N, T, K))
    c = coef(rng, 25.0); r = int(rng.integers(0, N)); c[r] = np.minimum(np.abs(c[r]), 127)
    return pack(j, c, x, y, a)
def setup_inputs_spread(rng):
    j, x, y, a = parts(rng)
    j = np.minimum((W * rng.random(j.shape) ** 3).astype(np.int64), W - 1); a = np.minimum((W * rng.random(a.shape) ** 3).astype(np.int64), W - 1)
    c = np.exp2(8.0 * rng.random((N, 8, 1, W))) * (0.5 * rng.standard_normal((N, 8, 16, W)) + 0.25)
    x = np.minimum((17 * rng.random(x.shape) ** 2).astype(np.int64), EMPTY); y = np.minimum((16 * rng.random(y.shape) ** 2).astype(np.int64), 15)
    return pack(j, np.minimum(np.maximum(np.rint(c), -128), 127), x, y, a)
def check_inputs(d):
    bad = []
    for k, lo, hi in (("jm", 0, W - 1), ("cf", -128, 127), ("lt", 0, 16), ("y0", 0, 15), ("st", 0, W - 1)):
        a = np.asarray(d[k]).astype(np.float32)
        if not (np.all(a == np.floor(a)) and np.min(a) >= lo and np.max(a) <= hi): bad.append("range of " + k)
        if np.any(np.signbit(a) & (a == 0)): bad.append("-0.0 in " + k)
    return bad
def reference(jm, cf, lt, y0, st):
    J = jm.astype(np.int64).reshape(N, 8, 16, W); C = cf.astype(np.float32).astype(np.int64).reshape(N, 8, 16, W)
    x = lt.astype(np.float32).astype(np.int64).reshape(N, 8, N, L, K); y = y0.astype(np.float32).astype(np.int64)
    start = np.stack([gentries(a) for a in st]).astype(np.int64).reshape(N, 8, T, K)
    new = np.full((N, 8, T, K), EMPTY, np.int64); v = np.zeros((N, 8, 16, K), np.int64); g = np.arange(8)[:, None]
    for t in range(T):
        for s in range(N):
            b = J[s][g, y[s], start[s, :, t]]; u = np.take_along_axis(C[s], b[:, None, :], 2)
            live = np.ones((8, K), bool)
            for d in range(N):
                q = (s + d) % N
                slots = [new[s, :, i] for i in range(t - 1, -1, -1)] if d == 0 else []
                for z in slots + [x[q, :, s, l] for l in range(L)]:
                    go = live & (z < EMPTY)
                    b = np.where(go, J[q][g, np.minimum(z, 15), b], b)
                    w = np.minimum(np.maximum(u + np.take_along_axis(C[q], b[:, None, :], 2), -TOP), TOP)
                    u = np.where(go[:, None, :], w, u)
                    hit = go & (np.add.reduce((u < 0).astype(np.int64), axis=1) >= NEG)
                    z[hit] = EMPTY; live = live & ~hit
            new[s, :, t] = np.where(live, y[s], EMPTY)
            y[s] = np.argmax(u, axis=1)
            v[s] = u
    return {"yl": x.reshape(N, 8, N * L * K).astype(np.float32).astype(BF), "yi": new.reshape(N, 8, T * K).astype(np.float32).astype(BF), "yv": v.reshape(N, 128, K).astype(np.float32).astype(BF)}

@@ -1,0 +1,515 @@
+from concourse.mybir import AluOpType as A, ActivationFunctionType as F
+
+N, K, TW, W = 4, 1024, 3, 4608
+HALF = K // 2
+NC = K // 16
+SH = 16
+WIN = SH + 5120
+PH = 2048
+OFF = float(SH + PH)
+FLAG = -16384.0
+BYSCALAR = ()
+LEAD = 3.0
+NU, NF, NB, NH = 40, 64, 64, 30
+
+SCRATCH = {
+    "jint": ("sbuf", [128, W], "int32"), "jw": ("sbuf", [128, WIN], "float32"),
+    "cw": ("sbuf", [128, WIN], "bfloat16"), "cw3": ("sbuf", [128, WIN], "bfloat16"), "cst": ("sbuf", [128, 512], "bfloat16"),
+    "ltn": ("sbuf", [8, N * K], "bfloat16"), "y0n": ("sbuf", [8, K], "bfloat16"),
+    "sti": ("sbuf", [128, TW * NC], "int32"), "sta": ("sbuf", [128, TW * NC], "float32"),
+    "stb": ("sbuf", [128, TW * NC], "float32"), "stu": ("sbuf", [128, TW * NC], "uint16"),
+    "eb": ("sbuf", [128, 2048], "bfloat16"), "blk": ("sbuf", [128, 128], "bfloat16"),
+    "idb": ("sbuf", [128, 128], "bfloat16"), "idn": ("sbuf", [128, 128], "bfloat16"), "idm": ("sbuf", [128, 128], "bfloat16"),
+    "hx": ("sbuf", [128, 128], "bfloat16"), "gx": ("sbuf", [8, 2048], "bfloat16"), "bc8": ("sbuf", [8, 128], "bfloat16"),
+    "pidx": ("sbuf", [128, 1], "int32"), "pxi": ("sbuf", [128, 1], "int32"), "xcol": ("sbuf", [128, 1], "float32"),
+    "negx": ("sbuf", [128, 1], "float32"), "ecol": ("sbuf", [128, 1], "float32"),
+    "jl0": ("sbuf", [128, NC], "float32"), "jl": ("sbuf", [128, NC], "float16"), "dl": ("sbuf", [128, HALF], "float32"),
+    "lu": ("sbuf", [128, NC * NU], "uint16"), "lf": ("sbuf", [128, NC * NF], "float32"),
+    "lb": ("sbuf", [128, NC * NB], "bfloat16"), "lh": ("sbuf", [128, NC * NH], "float16"),
+    "l0n": ("sbuf", [128, NC * N], "bfloat16"), "zn0": ("sbuf", [128, NC * N], "bfloat16"), "absn": ("sbuf", [128, NC * N], "float32"),
+    "run0": ("sbuf", [128, HALF], "float32"), "run1": ("sbuf", [128, HALF], "float32"),
+    "mi": ("sbuf", [128, 32 * 4], "int32"), "me": ("sbuf", [128, 32 * 4], "bfloat16"),
+    "gh0": ("sbuf", [128, HALF], "bfloat16"), "gh1": ("sbuf", [128, HALF], "bfloat16"),
+}
+BANKS = ("xa0", "xa1", "xc", "kt0", "kt1", "nt0", "nt1", "ms")
+for _i in BANKS:
+    SCRATCH[_i] = ("psum", [128, 512], "float32")
+for _i in range(N):
+    SCRATCH["mk%d" % _i] = ("sbuf", [128, K], "bfloat16")
+for _i in range(3):
+    SCRATCH["my%d" % _i] = ("sbuf", [128, K], "bfloat16")
+    SCRATCH["mt%d" % _i] = ("sbuf", [128, HALF], "bfloat16")
+    SCRATCH["md%d" % _i] = ("sbuf", [128, K], "float16")
+    for _n in ("v", "tm", "sg"):
+        SCRATCH[_n + str(_i)] = ("sbuf", [128, K], "bfloat16")
+for _i in range(7):
+    SCRATCH["no%d" % _i] = ("sbuf", [8, K], "bfloat16")
+for _i in range(2):
+    SCRATCH["yn%d" % _i] = ("sbuf", [8, K], "bfloat16")
+SEMAPHORES = ["vq", "sq", "pq", "gq", "snt", "rcw"] + ["ld%d" % i for i in range(10)] + ["st%d" % i for i in range(8)]
+for _d in range(1, N):
+    SCRATCH["zi%d" % _d] = ("sbuf", [128, NC], "bfloat16")
+    SEMAPHORES.append("rzi%d" % _d)
+for _t in range(TW):
+    SCRATCH["bh%d" % _t] = ("sbuf", [128, NC], "float16")
+    SEMAPHORES.append("rh%d" % _t)
+    for _d in range(1, N):
+        _x = "%d%d" % (_t, _d)
+        SCRATCH["br" + _x] = ("sbuf", [128, NC], "uint16")
+        SCRATCH["fr" + _x] = ("sbuf", [128, NC], "bfloat16")
+        SEMAPHORES += ["rb" + _x, "rf" + _x]
+        if _d < N - 1:
+            SCRATCH["cg" + _x] = ("sbuf", [128, 2 * (SH + HALF)], "bfloat16")
+            SCRATCH["cs" + _x] = ("sbuf", [128, SH + K], "bfloat16")
+            SEMAPHORES.append("rc" + _x)
+
+
+def add(pl, eng, cost, reads, writes, fn, sem=None, lat=0.0, inc=None, after=None, kind="c"):
+    tasks, last, rd = pl["tasks"], pl["last"], pl["rd"]
+    i = len(tasks)
+    deps = set(last[k] for k in list(reads) + list(writes) if k in last)
+    for k in reads:
+        if k in BANKS:
+            deps |= set(j for j in rd.get(k, []) if tasks[j]["eng"] != eng)
+    for k in writes:
+        deps |= set(rd.get(k, []))
+    for k in reads:
+        rd.setdefault(k, []).append(i)
+    for k in writes:
+        last[k] = i
+        rd[k] = []
+    tdeps = deps if after is None else deps | set([after])
+    tasks.append({"eng": eng, "cost": cost, "deps": sorted(deps), "tdeps": sorted(tdeps), "fn": fn, "sem": sem, "lat": lat,
+                  "inc": inc, "kind": kind, "lead": pl["lead"]})
+    return i
+
+
+def order(tasks):
+    n = len(tasks)
+    succ = [[] for _ in range(n)]
+    for i in range(n):
+        for j in tasks[i]["tdeps"]:
+            succ[j].append(i)
+    pri = [0.0] * n
+    own = [0.0] * n
+    for i in range(n - 1, -1, -1):
+        pri[i] = max([pri[j] for j in succ[i]] + [0.0]) + tasks[i]["cost"] + tasks[i]["lat"]
+        own[i] = 1e6 - i if "first" in tasks[i] else pri[i] + tasks[i]["lead"]
+    left = [len(tasks[i]["tdeps"]) for i in range(n)]
+    rt = [0.0] * n
+    todo = [i for i in range(n) if left[i] == 0]
+    busy = {}
+    start = [0.0] * n
+    while todo:
+        i = max(todo, key=lambda a: (own[a], -a))
+        todo.remove(i)
+        e, c = tasks[i]["eng"], tasks[i]["cost"]
+        s = rt[i]
+        if e != "R":
+            b = busy.setdefault(e, [])
+            k = 0
+            while k < len(b) and b[k][1] <= s:
+                k += 1
+            while k < len(b) and b[k][0] < s + c:
+                s = max(s, b[k][1])
+                k += 1
+            b.insert(k, (s, s + c))
+        start[i] = s
+        for j in succ[i]:
+            left[j] -= 1
+            rt[j] = max(rt[j], s + c + tasks[i]["lat"] + (0.03 if tasks[j]["eng"] == e else 0.08))
+            if left[j] == 0:
+                todo.append(j)
+    return sorted(range(n), key=lambda a: (start[a], a))
+
+
+def emit(g, T, tasks):
+    seq = order(tasks)
+    pos = dict((a, b) for b, a in enumerate(seq))
+    q = {"V": g.vector, "S": g.scalar, "P": g.tensor, "G": g, "Y": g.sync}
+    qsem = {"V": "vq", "S": "sq", "P": "pq", "G": "gq"}
+    count = {}
+    known = dict((e, {}) for e in q)
+    tok = {}
+    know = {}
+    for i in seq:
+        t = tasks[i]
+        e = t["eng"]
+        if e == "R":
+            tok[i] = (t["sem"], t["inc"])
+            know[i] = {t["sem"]: t["inc"]}
+            continue
+        kn = known[e]
+        for j in sorted(t["deps"], key=lambda a: -pos[a]):
+            s, v = tok[j]
+            if kn.get(s, 0) >= v:
+                continue
+            q[e].wait_ge(T.sem[s], v)
+            for s2 in know[j]:
+                kn[s2] = max(kn.get(s2, 0), know[j][s2])
+        ins = t["fn"]()
+        if t["kind"] == "c":
+            s = qsem[e]
+            for x in ins:
+                x.then_inc(T.sem[s], 1)
+            count[s] = count.get(s, 0) + len(ins)
+        elif t["kind"] == "d":
+            s = t["sem"]
+            ins[0].then_inc(T.sem[s], 16)
+            count[s] = 16
+        else:
+            s = "snt"
+            count[s] = count.get(s, 0) + t["inc"]
+        tok[i] = (s, count[s])
+        know[i] = dict(kn)
+        know[i][s] = count[s]
+    for s in count:
+        if known["G"].get(s, 0) < count[s]:
+            g.wait_ge(T.sem[s], count[s])
+
+
+def rank_program(g, core, T, topo):
+    rank = T.rank_of(core)
+    if rank is None:
+        return
+    pl = {"tasks": [], "last": {}, "rd": {}, "lead": 0.0}
+    vec, sca, ten, syn = g.vector, g.scalar, g.tensor, g.sync
+    cores = T.cores
+    used = {}
+
+    def take(kind):
+        used[kind] = used.get(kind, -1) + 1
+        return used[kind]
+
+    def new(buf):
+        n = take(buf)
+        t = T[buf]
+        return (t[:, NC * n:NC * n + NC], "%s.%d" % (buf, n), [t[:, NC * n + 32 * h:NC * n + 32 * h + 32] for h in range(2)])
+
+    def rot(kind, n=3):
+        return kind + str(take(kind) % n)
+
+    def vts(out, ok, in0, ik, s1, s2, op0, op1, cost=0.08, more=()):
+        args = (out, in0, s1, s2, op0) if op1 is None else (out, in0, s1, s2, op0, op1)
+        return add(pl, "V", cost, [ik] + list(more), [ok], lambda: [vec.tensor_scalar(*args)])
+
+    def vtt(out, ok, a, ak, b, bk, op, cost=0.08):
+        return add(pl, "V", cost, [ak, bk], [ok], lambda: [vec.tensor_tensor(out, a, b, op)])
+
+    def vcp(out, ok, a, ak, cost=0.08):
+        return add(pl, "V", cost, [ak], [ok], lambda: [vec.tensor_copy(out, a)])
+
+    def act(out, ok, in_, reads, func, cost, **kw):
+        return add(pl, "S", cost, reads, [ok], lambda: [sca.activation(out, in_, func, **kw)])
+
+    def mm(group, reads, writes, cost):
+        return add(pl, "P", cost, reads, writes, lambda: [ten.matmul(*x) for x in group])
+
+    def memset(ap, key, c, cost=0.08):
+        return add(pl, "V", cost, [], [key], lambda: [vec.memset(ap, c)])
+
+    def send(out, in_, sem, to, reads, key, lat, bulk=False):
+        dst = cores[to]
+        rid, pid, _ = topo.addr(dst)
+        en = topo.engines(core, dst)
+        n = len(en) // 2
+        m = sum(1 << x for x in (en[n:] if bulk else en[:n]))
+        i = add(pl, "G", 0.4, reads, [], lambda: [g.remote_dma(out, in_, T.sem[sem], T.sem.snt, pid, rid, m)], inc=n, kind="r")
+        return lambda: add(pl, "R", 0.0, [], key, None, sem=sem, inc=n, after=i, lat=lat)
+
+    def load(eng, out, in_, key, lat):
+        qq = syn if eng == "Y" else sca
+        i = add(pl, eng, 0.1, [], [key], lambda: [qq.dma_start(out, in_)], sem="ld%d" % take("ld"), lat=lat, kind="d")
+        pl["tasks"][i]["first"] = True
+
+    def store(out, in_, reads):
+        add(pl, "Y", 0.1, reads, [], lambda: [syn.dma_start(out, in_)], sem="st%d" % take("st"), lat=2.0, kind="d")
+
+    def halves(k):
+        return [k + ".0", k + ".1"]
+
+    HS = [slice(0, HALF), slice(HALF, K)]
+
+    load("S", T.y0n[:], T.y0[:], "y0n", 3.0)
+    load("S", T.sti[:], T.st[:], "sti", 8.0)
+    load("S", T.ltn[:], T.lt[:], "ltn", 5.0)
+    at = 2.0
+    for p in range(5):
+        a, b = 1024 * p, min(W, 1024 * p + 1024)
+        at += (b - a) * 512 / 2.2e5
+        load("Y", T.jint[:, a:b], T.jm[:, a:b], "jint%d" % p, at)
+    load("Y", T.cst[:], T.cf[:, 4096:W], "cst", at + 0.9)
+    load("Y", T.cw[:, SH:SH + 4096], T.cf[:, 0:4096], "cwa", at + 5.4)
+
+    def gsel(ap, key, pat, op, base, cm, cost=0.42, after=None):
+        return add(pl, "G", cost, [key], [key], lambda: [g.affine_select(ap, ap, pat, op, 0.0, base, cm)], after=after)
+    memset(T.idb[:], "idb", 1.0, 0.15)
+    memset(T.blk[:], "blk", 1.0, 0.15)
+    memset(T.bc8[:], "bc8", 1.0, 0.15)
+    memset(T.eb[:], "eb", 0.0, 0.9)
+    memset(T.gx[:], "gx", 1.0, 0.9)
+    memset(T.hx[:], "hx", -1.0 / 1024.0, 0.15)
+    add(pl, "G", 0.14, [], ["pidx"], lambda: [g.iota(T.pidx[:], [[1, 1]], 0, 1)])
+    gsel(T.blk[:], "blk", [[-16, 8], [0, 16]], A.is_ge, 0, 1)
+    i = gsel(T.blk[:], "blk", [[16, 8], [0, 16]], A.is_ge, 15, -1)
+    gsel(T.bc8[:], "bc8", [[-1, 8], [0, 16]], A.is_equal, 0, 1)
+    i = gsel(T.idb[:], "idb", [[-1, 128]], A.is_equal, 0, 1, 0.42, i)
+    add(pl, "G", 0.25, [], ["jl0"], lambda: [g.iota(T.jl0[:], [[0, 2], [16, NC // 2]], -PH, 0, allow_small_or_imprecise_dtypes=True)])
+    gsel(T.hx[:], "hx", [[-1, 16], [-16, 8]], A.is_equal, 0, 1, 0.42, i)
+    gsel(T.gx[:], "gx", [[1, 16], [-16, 8], [-1, 16]], A.is_equal, 0, 16, 3.6, i)
+
+    add(pl, "V", 0.06, ["pidx"], ["pxi"], lambda: [vec.tensor_scalar(T.pxi[:], T.pidx[:], 15, None, A.bitwise_and)])
+    vcp(T.xcol[:], "xcol", T.pxi[:], "pxi")
+    vts(T.negx[:], "negx", T.xcol[:], "xcol", -1.0, None, A.mult, None)
+    vts(T.ecol[:], "ecol", T.xcol[:], "xcol", -1.0 / 16.0, 15.0 / 16.0, A.mult, A.add)
+    vts(T.jl[:], "jl", T.jl0[:], "jl0", T.xcol[:, 0:1], None, A.add, None, more=["xcol"])
+    add(pl, "S", 1.3, ["blk"], ["eb"],
+        lambda: [sca.activation(T.eb[:, 128 * x + x:128 * x + 128:16], T.blk[:, x:128:16], F.Copy) for x in range(16)])
+    vts(T.idn[:], "idn", T.idb[:], "idb", -1.0, None, A.mult, None, 0.12)
+    vts(T.idm[:], "idm", T.idb[:], "idb", -0.5, None, A.mult, None, 0.12)
+    memset(T.dl[:], "dl", 1.0 / 16.0, 0.45)
+    memset(T.dl[:, 0:HALF:16], "dl", -1000.0)
+    memset(T.jw[:, 0:SH], "jwz", 0.0)
+    memset(T.jw[:, SH + 4096:WIN], "jwu", 0.0, 0.9)
+    memset(T.cw[:, 0:SH], "cwz", 0.0)
+    memset(T.cw[:, SH + 4096:WIN], "cwu", 0.0, 0.5)
+    for t in range(TW):
+        for d in range(1, N - 1):
+            x = "%d%d" % (t, d)
+            memset(T["cg" + x][:, 0:SH], "cgz" + x, 0.0)
+            memset(T["cs" + x][:, HALF:HALF + SH], "csz" + x, 0.0)
+
+    for h in range(2):
+        nt = "nt%d" % h
+        mm([(T[nt][:, 0:HALF], T.bc8[:], T.y0n[:, HS[h]], True, True)], ["bc8", "y0n"], [nt], 0.35)
+        vts(T.my0[:, HS[h]], "my0.%d" % h, T[nt][:, 0:HALF], nt, T.xcol[:, 0:1], None, A.is_equal, None, 0.5, ["xcol"])
+    mm([(T.ms[:, 0:256], T.gx[:, 128 * r:128 * r + 128], T.ltn[:, r:N * K:16], r == 0, r == 15) for r in range(16)],
+       ["gx", "ltn"], ["ms"], 2.5)
+    vts(T.zn0[:], "zn0", T.ms[:, 0:256], "ms", 15.5, FLAG, A.is_ge, A.mult, 0.25)
+    vts(T.absn[:], "absn", T.ms[:, 0:256], "ms", 15.5, None, A.is_ge, None, 0.25)
+    vts(T.l0n[:], "l0n", T.ms[:, 0:256], "ms", -1024.0, None, A.mult, None, 0.25)
+    for d in range(N):
+        for h in range(2):
+            bk = ("xa0", "xa1", "xc")[take("mb") % 3]
+            mt = rot("mt")
+            c = ((rank - d) % N) * K + HALF * h
+            mm([(T[bk][:, 0:HALF], T.bc8[:], T.ltn[:, c:c + HALF], True, True)], ["bc8", "ltn"], [bk], 0.35)
+            act(T[mt][:], mt, T[bk][:, 0:HALF], [bk, "negx"], F.Abs, 0.5, bias=T.negx[:, 0:1])
+            act(T["mk%d" % d][:, HS[h]], "mk%d.%d" % (d, h), T[mt][:], [mt], F.Relu, 0.5, bias=1.0, scale=-1.0)
+    for d in range(1, N):
+        s = (rank - d) % N
+        send(T["zi%d" % d][:], T.zn0[:, NC * s:NC * s + NC], "rzi%d" % d, s, ["zn0"], ["zi%d" % d], 2.0)()
+
+    vts(T.sta[:], "sta", T.sti[:], "sti", 2.0, -4096.0, A.mult, A.add, 0.2)
+    vtt(T.stb[:], "stb", T.sti[:], "sti", T.sta[:], "sta", A.max, 0.35)
+    vts(T.stu[:], "stu", T.stb[:], "stb", float(SH), None, A.add, None, 0.2)
+    for p in range(9):
+        bk = "kt%d" % (p % 2)
+        a = 512 * p
+        src, ik = T.jint[:, a:a + 512], "jint%d" % (p // 2)
+        vts(T[bk][:], bk, src, ik, 4096.0, -6144.0, A.max, A.add, 0.48)
+        out, ok = (T.jw[:, SH + a:SH + a + 512], "jw%d" % p) if p < 8 else (T.jw[:, SH + 4096:WIN:2], "jwu")
+        vtt(out, ok, src, ik, T[bk][:], bk, A.add, 0.48)
+    JW = ["jwz", "jwu"] + ["jw%d" % p for p in range(8)]
+    act(T.cw[:, SH + 4096:WIN:2], "cwu", T.cst[:], ["cst"], F.Copy, 0.48)
+    CW = ["cwz", "cwu", "cwa"]
+    send(T.cw3[:], T.cw[:], "rcw", (rank + 1) % N, CW, ["cw3"], 9.0, True)()
+
+    def image(lst, lk, mask, mkeys, keep=None):
+        md = rot("md")
+        add(pl, "V", 1.65, JW + [lk] + mkeys, [md], lambda: [vec.tensor_tensor(T[md][:], T.jw[:].indirect(lst), mask[:], A.mult)])
+        bk = rot("xa", 2)
+        x = T[bk][:, 0:NC]
+        grp = [(x, T.eb[:, 128 * r:128 * r + 128], T[md][:, r:K:16], r == 0, r == 15 and keep is None) for r in range(16)]
+        if keep is not None:
+            grp.append((x, T.idb[:], keep[0], False, True))
+        mm(grp, ["eb", "idb", md] + ([keep[1]] if keep is not None else []), [bk], 0.65)
+        return x, bk
+
+    def tolist(x, xk):
+        l = new("lu")
+        vts(l[0], l[1], x, xk, OFF, 0.0, A.add, A.max)
+        return l
+
+    def bslot(lst, lk, mask, mkeys, absent, present, prev, want, wantl):
+        if prev is None:
+            prev = new("lf")
+            vts(prev[0], prev[1], lst, lk, -OFF, None, A.add, None)
+        if present is None:
+            k = new("lh")
+            vtt(k[0], k[1], prev[0], prev[1], absent[0], absent[1], A.mult)
+            x = image(lst, lk, mask, mkeys, k)
+            l = tolist(x[0], x[1]) if wantl else None
+            b = None
+            if want:
+                b = new("lh")
+                vcp(b[0], b[1], x[0], x[1])
+            return b, l
+        k, a, b = new("lf"), new("lf"), new("lh")
+        vtt(k[0], k[1], prev[0], prev[1], absent[0], absent[1], A.mult)
+        x = image(lst, lk, mask, mkeys)
+        vtt(a[0], a[1], x[0], x[1], present[0], present[1], A.mult)
+        vtt(b[0], b[1], a[0], a[1], k[0], k[1], A.add)
+        return b, tolist(b[0], b[1]) if wantl else None
+
+    def flags(z, zk):
+        n, p = new("lf"), new("lf")
+        act(n[0], n[1], z, [zk], F.Copy, 0.15, scale=1.0 / FLAG)
+        act(p[0], p[1], z, [zk], F.Identity, 0.15, bias=1.0, scale=-1.0 / FLAG)
+        return n, p
+
+    def gather_c(out, okeys, l):
+        for h in range(2):
+            act(out[h], okeys[h], T.cw[:].indirect(l[2][h]), CW + [l[1]], F.Identity, 0.86)
+
+    def vslot(v, base, zn, dead, wins, wkeys, at):
+        u = T.xc[:, NC:2 * NC]
+        grp = [(u, T.idb[:], base[0], True, False), (u, T.idb[:], zn[0], False, dead is None)]
+        dk = [] if dead is None else [dead[1]]
+        if dead is not None:
+            grp.append((u, T.idb[:], dead[0], False, True))
+        mm(grp, ["idb", base[1], zn[1]] + dk, ["xc"], 0.1)
+        l = tolist(u, "xc")
+        tm, nv = rot("tm"), rot("v")
+        sg = "sg" + tm[2:]
+        for h in range(2):
+            c = HS[h]
+            vk, tk, sk, nk = ["%s.%d" % (x, h) for x in (v, tm, sg, nv)]
+            vi, src, srk, cl = T[v][:, c], T[tm][:, c], tk, 0.28
+            if h and at in BYSCALAR:
+                gh = rot("gh", 2)
+                act(T[gh][:], gh, wins[h].indirect(l[2][h]), wkeys(h) + [l[1]], F.Identity, 0.85)
+                src, srk, cl = T.kt1[:, 0:HALF], "kt1", 0.55
+                mm([(src, T.idb[:], vi, True, False), (src, T.idb[:], T[gh][:], False, True)], ["idb", vk, gh], [srk], 0.5)
+            else:
+                add(pl, "V", 0.83, wkeys(h) + [l[1], vk], [tk],
+                    lambda src=src, h=h, vi=vi: [vec.tensor_tensor(src, wins[h].indirect(l[2][h]), vi, A.add)])
+            act(T[sg][:, c], sk, src, [srk], F.Sign, 0.57, bias=0.5)
+            vts(T[nv][:, c], nk, src, srk, 255.0, -255.0, A.min, A.max, cl)
+        o = T.xc[:, 0:NC]
+        grp = [(o, T.idm[:], zn[0], True, False)]
+        if dead is not None:
+            grp.append((o, T.idb[:], dead[0], False, False))
+        grp += [(o, T.eb[:, 128 * r:128 * r + 128], T[sg][:, r:K:16], False, r == 15) for r in range(16)]
+        mm(grp, ["idm", "idb", zn[1], "eb"] + halves(sg) + dk, ["xc"], 0.7)
+        nd, nz = new("lb"), new("lb")
+        vts(nd[0], nd[1], o, "xc", -1.5, FLAG, A.is_le, A.mult)
+        if dead is None:
+            vtt(nz[0], nz[1], zn[0], zn[1], nd[0], nd[1], A.add)
+        else:
+            q = T.ms[:, 0:NC]
+            mm([(q, T.idb[:], zn[0], True, False), (q, T.idn[:], dead[0], False, False), (q, T.idb[:], nd[0], False, True)],
+               ["idb", "idn", zn[1], dead[1], nd[1]], ["ms"], 0.1)
+            act(nz[0], nz[1], q, ["ms"], F.Copy, 0.15)
+        return nv, nd, nz
+
+    def ylist(rows, keys, a, b):
+        l = new("lb")
+        mm([(T.ms[:, 0:NC], T.gx[:, 128 * r:128 * r + 128], rows[:, r:K:16], r == 0, r == 15) for r in range(16)],
+           ["gx"] + keys, ["ms"], 0.7)
+        vts(l[0], l[1], T.ms[:, 0:NC], "ms", a, b, A.mult, A.add)
+        return l
+
+    def letters(y, yk, z, zk, out, oc):
+        f = new("lb")
+        vtt(f[0], f[1], y, yk, z, zk, A.min)
+        no = rot("no", 7)
+        for h in range(2):
+            nt = "nt%d" % h
+            mm([(T[nt][0:8, r:512:16], T.hx[:, 8 * r:8 * r + 8], f[2][h], True, True) for r in range(16)], ["hx", f[1]], [nt], 0.4)
+            if h:
+                vcp(T[no][:, HS[h]], no + ".1", T[nt][0:8, :], nt, 0.55)
+            else:
+                act(T[no][:, HS[h]], no + ".0", T[nt][0:8, :], [nt], F.Copy, 0.57)
+        store(out[:, oc:oc + K], T[no][:], halves(no))
+
+    MY = [T.my0, T.my1, T.my2]
+    zn = [(T.zn0[:, NC * rank:NC * rank + NC], "zn0")] + [(T["zi%d" % d][:], "zi%d" % d) for d in range(1, N)]
+    res = []
+    ys = [ylist(T.y0n, ["y0n"], -1024.0, 0.0)]
+    for t in range(TW):
+        pl["lead"] = LEAD
+        x = image(T.stu[:, NC * t:NC * t + NC], "stu", MY[t], halves("my%d" % t))
+        l = lstart = tolist(x[0], x[1])
+        todo = [(MY[i], halves("my%d" % i), res[i]) for i in range(t - 1, -1, -1)] + [(T.mk0, halves("mk0"), zn[0])]
+        chain = []
+        prev = None
+        for mask, mkeys, z in todo:
+            n, p = flags(z[0], z[1]) if t else ((T.absn[:, NC * rank:NC * rank + NC], "absn"), None)
+            prev, l = bslot(l[0], l[1], mask, mkeys, n, p, prev, True, True)
+            chain.append(prev)
+        arrive = send(T["br%d1" % t][:], l[0], "rb%d1" % t, (rank + 1) % N, [l[1]], ["br%d1" % t], 1.9)
+        pl["lead"] = 0.0
+        v = rot("v")
+        gather_c([T[v][:, HS[0]], T[v][:, HS[1]]], halves(v), lstart)
+        dead = None
+        for j in range(len(todo)):
+            v, dead, nz = vslot(v, chain[j], todo[j][2], dead, [T.cw[:], T.cw[:]], lambda h: CW, (t, -j))
+            if j < t:
+                res[t - 1 - j] = nz
+            else:
+                zn[0] = nz
+        pend = []
+        for d in range(1, N):
+            x = "%d%d" % (t, d)
+            arrive()
+            home = (rank - d) % N
+            pl["lead"] = LEAD
+            n, p = flags(T["fr%d%d" % (t - 1, d)][:], "fr%d%d" % (t - 1, d)) if t else ((T.absn[:, NC * home:NC * home + NC], "absn"), None)
+            lastd = d == N - 1
+            b, l = bslot(T["br" + x][:], "br" + x, T["mk%d" % d], halves("mk%d" % d), n, p, None, lastd, not lastd)
+            if lastd:
+                pend.append(send(T["bh%d" % t][:], b[0], "rh%d" % t, home, [b[1]], ["bh%d" % t], 1.9))
+            else:
+                k = "%d%d" % (t, d + 1)
+                arrive = send(T["br" + k][:], l[0], "rb" + k, (rank + 1) % N, [l[1]], ["br" + k], 1.9)
+            pl["lead"] = 0.0
+            if not lastd:
+                cs = T["cs" + x]
+                gather_c([cs[:, 0:HALF], cs[:, SH + HALF:SH + K]], halves("cs" + x), l)
+                pend.append(send(T["cg" + x][:, SH:2 * (SH + HALF)], cs[:], "rc" + x, home, halves("cs" + x) + ["csz" + x],
+                                 halves("cg" + x), 3.0, True))
+        for f in pend:
+            f()
+        for d in range(1, N):
+            x = "%d%d" % (t, d)
+            if d == N - 1:
+                v, dead, nz = vslot(v, (T["bh%d" % t][:], "bh%d" % t), zn[d], dead, [T.cw3[:], T.cw3[:]], lambda h: ["cw3"], (t, d))
+            else:
+                cg = T["cg" + x]
+                v, dead, nz = vslot(v, (T.jl[:], "jl"), zn[d], dead, [cg[:, 0:SH + HALF], cg[:, SH + HALF:2 * (SH + HALF)]],
+                                    lambda h, x=x: ["cgz" + x if h == 0 else "cg%s.1" % x, "cg%s.%d" % (x, h)], (t, d))
+            zn[d] = nz
+            send(T["fr" + x][:], nz[0], "rf" + x, (rank + d) % N, [nz[1]], ["fr" + x], 2.0)()
+        res.append(dead)
+        if t < TW - 1:
+            yn = "yn%d" % t
+            for h in range(2):
+                kt, nt, ru = "kt%d" % h, "nt%d" % h, "run%d" % h
+                c0 = HALF * h
+                mm([(T[kt][:, 128 * k:128 * k + 128], T[v][:, c0 + 128 * k:c0 + 128 * k + 128], T.idb[:], True, True) for k in range(4)],
+                   ["%s.%d" % (v, h), "idb"], [kt], 0.35)
+                add(pl, "V", 0.5, ["dl", kt], [ru],
+                    lambda ru=ru, kt=kt: [vec.tensor_tensor_scan(T[ru][:], T.dl[:], T[kt][:], 0.0, A.add, A.max)])
+                q = 2 * t + h
+                mi, me = T.mi[:, 32 * q:32 * q + 32], T.me[:, 32 * q:32 * q + 32]
+                vts(mi, "mi%d" % q, T[ru][:, 15:HALF:16], ru, -15.0 / 32.0, None, A.add, None)
+                vtt(me, "me%d" % q, T[ru][:, 15:HALF:16], ru, mi, "mi%d" % q, A.subtract)
+                mm([(T[nt][0:8, 128 * k:128 * k + 128], T.me[:, 32 * q + 8 * k:32 * q + 8 * k + 8], T.idb[:], True, True) for k in range(4)],
+                   ["me%d" % q, "idb"], [nt], 0.35)
+                if h:
+                    vcp(T[yn][:, HS[h]], yn + ".1", T[nt][0:8, :], nt, 0.55)
+                else:
+                    act(T[yn][:, HS[h]], yn + ".0", T[nt][0:8, :], [nt], F.Copy, 0.57)
+                mm([(T[kt][:], T.bc8[:], T[yn][:, HS[h]], True, True)], ["bc8", "%s.%d" % (yn, h)], [kt], 0.35)
+                vts(MY[t + 1][:, HS[h]], "my%d.%d" % (t + 1, h), T[kt][:], kt, T.ecol[:, 0:1], None, A.is_equal, None, 0.48, ["ecol"])
+            ys.append(ylist(T[yn], halves(yn), 16384.0, -15360.0))
+
+    store(T.yv[:], T[v][:], halves(v))
+    for d in range(N):
+        s = (rank - d) % N
+        z = zn[0] if d == 0 else (T["fr%d%d" % (TW - 1, d)][:], "fr%d%d" % (TW - 1, d))
+        letters(T.l0n[:, NC * s:NC * s + NC], "l0n", z[0], z[1], T.yl, s * K)
+    for t in range(TW):
+        letters(ys[t][0], ys[t][1], res[t][0], res[t][1], T.yi, t * K)
+    emit(g, T, pl["tasks"])

@@ -8,8 +8,8 @@ WIN = SH + 5120
 PH = 2048
 OFF = float(SH + PH)
 FLAG = -16384.0
-BYSCALAR = ()
-LEAD = 3.0
+BYSCALAR = {(2, -2): (0, 1), (2, -1): (0, 1), (2, 0): (0, 1), (2, 1): (1,)}
+SIGNV = ((TW - 1, N - 1),)
 NU, NF, NB, NH = 40, 64, 64, 30
 
 SCRATCH = {
@@ -23,13 +23,13 @@ SCRATCH = {
     "hx": ("sbuf", [128, 128], "bfloat16"), "gx": ("sbuf", [8, 2048], "bfloat16"), "bc8": ("sbuf", [8, 128], "bfloat16"),
     "pidx": ("sbuf", [128, 1], "int32"), "pxi": ("sbuf", [128, 1], "int32"), "xcol": ("sbuf", [128, 1], "float32"),
     "negx": ("sbuf", [128, 1], "float32"), "ecol": ("sbuf", [128, 1], "float32"),
-    "jl0": ("sbuf", [128, NC], "float32"), "jl": ("sbuf", [128, NC], "float16"), "dl": ("sbuf", [128, HALF], "float32"),
+    "jl0": ("sbuf", [128, NC], "float32"), "jl": ("sbuf", [128, NC], "float16"),
+    "dl": ("sbuf", [128, HALF], "float32"), "ha": ("sbuf", [128, HALF], "bfloat16"),
     "lu": ("sbuf", [128, NC * NU], "uint16"), "lf": ("sbuf", [128, NC * NF], "float32"),
     "lb": ("sbuf", [128, NC * NB], "bfloat16"), "lh": ("sbuf", [128, NC * NH], "float16"),
     "l0n": ("sbuf", [128, NC * N], "bfloat16"), "zn0": ("sbuf", [128, NC * N], "bfloat16"), "absn": ("sbuf", [128, NC * N], "float32"),
-    "run0": ("sbuf", [128, HALF], "float32"), "run1": ("sbuf", [128, HALF], "float32"),
-    "mi": ("sbuf", [128, 32 * 4], "int32"), "me": ("sbuf", [128, 32 * 4], "bfloat16"),
-    "gh0": ("sbuf", [128, HALF], "bfloat16"), "gh1": ("sbuf", [128, HALF], "bfloat16"),
+    "mi": ("sbuf", [128, 32 * 4], "int32"),
+    "js1": ("sbuf", [128, K], "float32"), "js2": ("sbuf", [128, K], "float32"),
 }
 BANKS = ("xa0", "xa1", "xc", "kt0", "kt1", "nt0", "nt1", "ms")
 for _i in BANKS:
@@ -37,7 +37,6 @@ for _i in BANKS:
 for _i in range(N):
     SCRATCH["mk%d" % _i] = ("sbuf", [128, K], "bfloat16")
 for _i in range(3):
-    SCRATCH["my%d" % _i] = ("sbuf", [128, K], "bfloat16")
     SCRATCH["mt%d" % _i] = ("sbuf", [128, HALF], "bfloat16")
     SCRATCH["md%d" % _i] = ("sbuf", [128, K], "float16")
     for _n in ("v", "tm", "sg"):
@@ -45,7 +44,12 @@ for _i in range(3):
 for _i in range(7):
     SCRATCH["no%d" % _i] = ("sbuf", [8, K], "bfloat16")
 for _i in range(2):
+    SCRATCH["my%d" % _i] = ("sbuf", [128, K], "bfloat16")
     SCRATCH["yn%d" % _i] = ("sbuf", [8, K], "bfloat16")
+    SCRATCH["gh%d" % _i] = ("sbuf", [128, HALF], "bfloat16")
+    SCRATCH["run%d" % _i] = ("sbuf", [128, HALF], "float32")
+    SCRATCH["bz%d" % _i] = ("sbuf", [128, HALF], "bfloat16")
+    SCRATCH["hs%d" % _i] = ("sbuf", [128, HALF], "bfloat16")
 SEMAPHORES = ["vq", "sq", "pq", "gq", "snt", "rcw"] + ["ld%d" % i for i in range(10)] + ["st%d" % i for i in range(8)]
 for _d in range(1, N):
     SCRATCH["zi%d" % _d] = ("sbuf", [128, NC], "bfloat16")
@@ -61,7 +65,7 @@ for _t in range(TW):
         if _d < N - 1:
             SCRATCH["cg" + _x] = ("sbuf", [128, 2 * (SH + HALF)], "bfloat16")
             SCRATCH["cs" + _x] = ("sbuf", [128, SH + K], "bfloat16")
-            SEMAPHORES.append("rc" + _x)
+            SEMAPHORES += ["rc%s0" % _x, "rc%s1" % _x]
 
 
 def add(pl, eng, cost, reads, writes, fn, sem=None, lat=0.0, inc=None, after=None, kind="c"):
@@ -78,9 +82,10 @@ def add(pl, eng, cost, reads, writes, fn, sem=None, lat=0.0, inc=None, after=Non
     for k in writes:
         last[k] = i
         rd[k] = []
+    deps.discard(i)
     tdeps = deps if after is None else deps | set([after])
     tasks.append({"eng": eng, "cost": cost, "deps": sorted(deps), "tdeps": sorted(tdeps), "fn": fn, "sem": sem, "lat": lat,
-                  "inc": inc, "kind": kind, "lead": pl["lead"]})
+                  "inc": inc, "kind": kind})
     return i
 
 
@@ -94,7 +99,7 @@ def order(tasks):
     own = [0.0] * n
     for i in range(n - 1, -1, -1):
         pri[i] = max([pri[j] for j in succ[i]] + [0.0]) + tasks[i]["cost"] + tasks[i]["lat"]
-        own[i] = 1e6 - i if "first" in tasks[i] else pri[i] + tasks[i]["lead"]
+        own[i] = 1e6 - i if "first" in tasks[i] else pri[i]
     left = [len(tasks[i]["tdeps"]) for i in range(n)]
     rt = [0.0] * n
     todo = [i for i in range(n) if left[i] == 0]
@@ -172,7 +177,7 @@ def rank_program(g, core, T, topo):
     rank = T.rank_of(core)
     if rank is None:
         return
-    pl = {"tasks": [], "last": {}, "rd": {}, "lead": 0.0}
+    pl = {"tasks": [], "last": {}, "rd": {}}
     vec, sca, ten, syn = g.vector, g.scalar, g.tensor, g.sync
     cores = T.cores
     used = {}
@@ -202,6 +207,9 @@ def rank_program(g, core, T, topo):
     def act(out, ok, in_, reads, func, cost, **kw):
         return add(pl, "S", cost, reads, [ok], lambda: [sca.activation(out, in_, func, **kw)])
 
+    def scan(out, ok, d0, d0k, d1, d1k, op0, op1, cost):
+        return add(pl, "V", cost, [d0k, d1k], [ok], lambda: [vec.tensor_tensor_scan(out, d0, d1, 0.0, op0, op1)])
+
     def mm(group, reads, writes, cost):
         return add(pl, "P", cost, reads, writes, lambda: [ten.matmul(*x) for x in group])
 
@@ -212,8 +220,9 @@ def rank_program(g, core, T, topo):
         dst = cores[to]
         rid, pid, _ = topo.addr(dst)
         en = topo.engines(core, dst)
-        n = len(en) // 2
-        m = sum(1 << x for x in (en[n:] if bulk else en[:n]))
+        en = en[1::2] if bulk else en[0::2]
+        n = len(en)
+        m = sum(1 << x for x in en)
         i = add(pl, "G", 0.4, reads, [], lambda: [g.remote_dma(out, in_, T.sem[sem], T.sem.snt, pid, rid, m)], inc=n, kind="r")
         return lambda: add(pl, "R", 0.0, [], key, None, sem=sem, inc=n, after=i, lat=lat)
 
@@ -231,7 +240,7 @@ def rank_program(g, core, T, topo):
     HS = [slice(0, HALF), slice(HALF, K)]
 
     load("S", T.y0n[:], T.y0[:], "y0n", 3.0)
-    load("S", T.sti[:], T.st[:], "sti", 8.0)
+    load("S", T.sti[:], T.st[:], "sti", 3.2)
     load("S", T.ltn[:], T.lt[:], "ltn", 5.0)
     at = 2.0
     for p in range(5):
@@ -269,6 +278,10 @@ def rank_program(g, core, T, topo):
     vts(T.idm[:], "idm", T.idb[:], "idb", -0.5, None, A.mult, None, 0.12)
     memset(T.dl[:], "dl", 1.0 / 16.0, 0.45)
     memset(T.dl[:, 0:HALF:16], "dl", -1000.0)
+    memset(T.ha[:], "ha", 1.0, 0.3)
+    memset(T.ha[:, 0:HALF:16], "ha", 0.0)
+    memset(T.bz0[:], "bz0", 0.0, 0.3)
+    memset(T.bz1[:], "bz1", 0.0, 0.3)
     memset(T.jw[:, 0:SH], "jwz", 0.0)
     memset(T.jw[:, SH + 4096:WIN], "jwu", 0.0, 0.9)
     memset(T.cw[:, 0:SH], "cwz", 0.0)
@@ -315,16 +328,37 @@ def rank_program(g, core, T, topo):
     CW = ["cwz", "cwu", "cwa"]
     send(T.cw3[:], T.cw[:], "rcw", (rank + 1) % N, CW, ["cw3"], 9.0, True)()
 
-    def image(lst, lk, mask, mkeys, keep=None):
-        md = rot("md")
-        add(pl, "V", 1.65, JW + [lk] + mkeys, [md], lambda: [vec.tensor_tensor(T[md][:], T.jw[:].indirect(lst), mask[:], A.mult)])
+    def summed(md, keep=None):
         bk = rot("xa", 2)
         x = T[bk][:, 0:NC]
         grp = [(x, T.eb[:, 128 * r:128 * r + 128], T[md][:, r:K:16], r == 0, r == 15 and keep is None) for r in range(16)]
         if keep is not None:
             grp.append((x, T.idb[:], keep[0], False, True))
-        mm(grp, ["eb", "idb", md] + ([keep[1]] if keep is not None else []), [bk], 0.65)
+        mm(grp, ["eb", "idb"] + halves(md) + ([keep[1]] if keep is not None else []), [bk], 0.65)
         return x, bk
+
+    def image(lst, lk, mask, mkeys, keep=None):
+        md = rot("md")
+        add(pl, "V", 1.65, JW + [lk] + mkeys, halves(md), lambda: [vec.tensor_tensor(T[md][:], T.jw[:].indirect(lst), mask[:], A.mult)])
+        return summed(md, keep)
+
+    for t in range(1, TW):
+        for h in range(2):
+            c = NC * t + 32 * h
+            act(T["js%d" % t][:, HS[h]], "js%d.%d" % (t, h), T.jw[:].indirect(T.stu[:, c:c + 32]), JW + ["stu"], F.Identity, 0.86)
+
+    def start(t):
+        if t == 0:
+            return image(T.stu[:, 0:NC], "stu", T.my0, halves("my0"))
+        md = rot("md")
+        for h in range(2):
+            kt = "kt%d" % h
+            vtt(T[md][:, HS[h]], "%s.%d" % (md, h), T["js%d" % t][:, HS[h]], "js%d.%d" % (t, h), T[kt][:], kt, A.mult, 0.53)
+        x = summed(md)
+        if t < TW - 1:
+            for h in range(2):
+                act(T["my%d" % t][:, HS[h]], "my%d.%d" % (t, h), T["kt%d" % h][:], ["kt%d" % h], F.Copy, 0.57)
+        return x
 
     def tolist(x, xk):
         l = new("lu")
@@ -376,15 +410,18 @@ def rank_program(g, core, T, topo):
             c = HS[h]
             vk, tk, sk, nk = ["%s.%d" % (x, h) for x in (v, tm, sg, nv)]
             vi, src, srk, cl = T[v][:, c], T[tm][:, c], tk, 0.28
-            if h and at in BYSCALAR:
+            if h in BYSCALAR.get(at, ()):
                 gh = rot("gh", 2)
                 act(T[gh][:], gh, wins[h].indirect(l[2][h]), wkeys(h) + [l[1]], F.Identity, 0.85)
-                src, srk, cl = T.kt1[:, 0:HALF], "kt1", 0.55
+                src, srk, cl = T["kt%d" % h][:], "kt%d" % h, 0.55
                 mm([(src, T.idb[:], vi, True, False), (src, T.idb[:], T[gh][:], False, True)], ["idb", vk, gh], [srk], 0.5)
             else:
                 add(pl, "V", 0.83, wkeys(h) + [l[1], vk], [tk],
                     lambda src=src, h=h, vi=vi: [vec.tensor_tensor(src, wins[h].indirect(l[2][h]), vi, A.add)])
-            act(T[sg][:, c], sk, src, [srk], F.Sign, 0.57, bias=0.5)
+            if h and at in SIGNV:
+                vts(T[sg][:, c], sk, src, srk, 0.0, 0.5, A.is_ge, A.subtract, 0.28)
+            else:
+                act(T[sg][:, c], sk, src, [srk], F.Sign, 0.57, bias=0.5)
             vts(T[nv][:, c], nk, src, srk, 255.0, -255.0, A.min, A.max, cl)
         o = T.xc[:, 0:NC]
         grp = [(o, T.idm[:], zn[0], True, False)]
@@ -393,9 +430,13 @@ def rank_program(g, core, T, topo):
         grp += [(o, T.eb[:, 128 * r:128 * r + 128], T[sg][:, r:K:16], False, r == 15) for r in range(16)]
         mm(grp, ["idm", "idb", zn[1], "eb"] + halves(sg) + dk, ["xc"], 0.7)
         nd, nz = new("lb"), new("lb")
-        vts(nd[0], nd[1], o, "xc", -1.5, FLAG, A.is_le, A.mult)
+        vts(nd[0], nd[1], o, "xc", -0.25, FLAG, A.is_le, A.mult)
         if dead is None:
             vtt(nz[0], nz[1], zn[0], zn[1], nd[0], nd[1], A.add)
+        elif at == (TW - 1, N - 1):
+            zd = new("lb")
+            vtt(zd[0], zd[1], zn[0], zn[1], dead[0], dead[1], A.subtract)
+            vtt(nz[0], nz[1], zd[0], zd[1], nd[0], nd[1], A.add)
         else:
             q = T.ms[:, 0:NC]
             mm([(q, T.idb[:], zn[0], True, False), (q, T.idn[:], dead[0], False, False), (q, T.idb[:], nd[0], False, True)],
@@ -410,12 +451,12 @@ def rank_program(g, core, T, topo):
         vts(l[0], l[1], T.ms[:, 0:NC], "ms", a, b, A.mult, A.add)
         return l
 
-    def letters(y, yk, z, zk, out, oc):
+    def letters(y, yk, z, zk, out, oc, bank="nt"):
         f = new("lb")
         vtt(f[0], f[1], y, yk, z, zk, A.min)
         no = rot("no", 7)
         for h in range(2):
-            nt = "nt%d" % h
+            nt = bank + str(h)
             mm([(T[nt][0:8, r:512:16], T.hx[:, 8 * r:8 * r + 8], f[2][h], True, True) for r in range(16)], ["hx", f[1]], [nt], 0.4)
             if h:
                 vcp(T[no][:, HS[h]], no + ".1", T[nt][0:8, :], nt, 0.55)
@@ -423,15 +464,13 @@ def rank_program(g, core, T, topo):
                 act(T[no][:, HS[h]], no + ".0", T[nt][0:8, :], [nt], F.Copy, 0.57)
         store(out[:, oc:oc + K], T[no][:], halves(no))
 
-    MY = [T.my0, T.my1, T.my2]
     zn = [(T.zn0[:, NC * rank:NC * rank + NC], "zn0")] + [(T["zi%d" % d][:], "zi%d" % d) for d in range(1, N)]
     res = []
     ys = [ylist(T.y0n, ["y0n"], -1024.0, 0.0)]
     for t in range(TW):
-        pl["lead"] = LEAD
-        x = image(T.stu[:, NC * t:NC * t + NC], "stu", MY[t], halves("my%d" % t))
+        x = start(t)
         l = lstart = tolist(x[0], x[1])
-        todo = [(MY[i], halves("my%d" % i), res[i]) for i in range(t - 1, -1, -1)] + [(T.mk0, halves("mk0"), zn[0])]
+        todo = [(T["my%d" % i], halves("my%d" % i), res[i]) for i in range(t - 1, -1, -1)] + [(T.mk0, halves("mk0"), zn[0])]
         chain = []
         prev = None
         for mask, mkeys, z in todo:
@@ -439,7 +478,6 @@ def rank_program(g, core, T, topo):
             prev, l = bslot(l[0], l[1], mask, mkeys, n, p, prev, True, True)
             chain.append(prev)
         arrive = send(T["br%d1" % t][:], l[0], "rb%d1" % t, (rank + 1) % N, [l[1]], ["br%d1" % t], 1.9)
-        pl["lead"] = 0.0
         v = rot("v")
         gather_c([T[v][:, HS[0]], T[v][:, HS[1]]], halves(v), lstart)
         dead = None
@@ -454,21 +492,21 @@ def rank_program(g, core, T, topo):
             x = "%d%d" % (t, d)
             arrive()
             home = (rank - d) % N
-            pl["lead"] = LEAD
             n, p = flags(T["fr%d%d" % (t - 1, d)][:], "fr%d%d" % (t - 1, d)) if t else ((T.absn[:, NC * home:NC * home + NC], "absn"), None)
             lastd = d == N - 1
             b, l = bslot(T["br" + x][:], "br" + x, T["mk%d" % d], halves("mk%d" % d), n, p, None, lastd, not lastd)
             if lastd:
                 pend.append(send(T["bh%d" % t][:], b[0], "rh%d" % t, home, [b[1]], ["bh%d" % t], 1.9))
+                continue
+            k = "%d%d" % (t, d + 1)
+            arrive = send(T["br" + k][:], l[0], "rb" + k, (rank + 1) % N, [l[1]], ["br" + k], 1.9)
+            cs, cg, ck, ak = T["cs" + x], T["cg" + x], halves("cs" + x), halves("cg" + x)
+            gather_c([cs[:, 0:HALF], cs[:, SH + HALF:SH + K]], ck, l)
+            if d == N - 2:
+                pend.append(send(cg[:, SH:SH + HALF], cs[:, 0:HALF], "rc%s0" % x, home, ck[:1], ak[:1], 2.6, True))
+                pend.append(send(cg[:, SH + HALF:2 * (SH + HALF)], cs[:, HALF:SH + K], "rc%s1" % x, home, [ck[1], "csz" + x], ak[1:], 2.6, True))
             else:
-                k = "%d%d" % (t, d + 1)
-                arrive = send(T["br" + k][:], l[0], "rb" + k, (rank + 1) % N, [l[1]], ["br" + k], 1.9)
-            pl["lead"] = 0.0
-            if not lastd:
-                cs = T["cs" + x]
-                gather_c([cs[:, 0:HALF], cs[:, SH + HALF:SH + K]], halves("cs" + x), l)
-                pend.append(send(T["cg" + x][:, SH:2 * (SH + HALF)], cs[:], "rc" + x, home, halves("cs" + x) + ["csz" + x],
-                                 halves("cg" + x), 3.0, True))
+                pend.append(send(cg[:, SH:2 * (SH + HALF)], cs[:], "rc%s0" % x, home, ck + ["csz" + x], ak, 3.0, True))
         for f in pend:
             f()
         for d in range(1, N):
@@ -489,27 +527,30 @@ def rank_program(g, core, T, topo):
                 c0 = HALF * h
                 mm([(T[kt][:, 128 * k:128 * k + 128], T[v][:, c0 + 128 * k:c0 + 128 * k + 128], T.idb[:], True, True) for k in range(4)],
                    ["%s.%d" % (v, h), "idb"], [kt], 0.35)
-                add(pl, "V", 0.5, ["dl", kt], [ru],
-                    lambda ru=ru, kt=kt: [vec.tensor_tensor_scan(T[ru][:], T.dl[:], T[kt][:], 0.0, A.add, A.max)])
+                scan(T[ru][:], ru, T.dl[:], "dl", T[kt][:], kt, A.add, A.max, 0.5)
                 q = 2 * t + h
-                mi, me = T.mi[:, 32 * q:32 * q + 32], T.me[:, 32 * q:32 * q + 32]
+                mi, bz, hs = T.mi[:, 32 * q:32 * q + 32], T["bz%d" % h], T["hs%d" % h]
                 vts(mi, "mi%d" % q, T[ru][:, 15:HALF:16], ru, -15.0 / 32.0, None, A.add, None)
-                vtt(me, "me%d" % q, T[ru][:, 15:HALF:16], ru, mi, "mi%d" % q, A.subtract)
-                mm([(T[nt][0:8, 128 * k:128 * k + 128], T.me[:, 32 * q + 8 * k:32 * q + 8 * k + 8], T.idb[:], True, True) for k in range(4)],
-                   ["me%d" % q, "idb"], [nt], 0.35)
-                if h:
-                    vcp(T[yn][:, HS[h]], yn + ".1", T[nt][0:8, :], nt, 0.55)
-                else:
-                    act(T[yn][:, HS[h]], yn + ".0", T[nt][0:8, :], [nt], F.Copy, 0.57)
-                mm([(T[kt][:], T.bc8[:], T[yn][:, HS[h]], True, True)], ["bc8", "%s.%d" % (yn, h)], [kt], 0.35)
-                vts(MY[t + 1][:, HS[h]], "my%d.%d" % (t + 1, h), T[kt][:], kt, T.ecol[:, 0:1], None, A.is_equal, None, 0.48, ["ecol"])
+                vtt(bz[:, 0:HALF:16], "bz%d" % h, T[ru][:, 15:HALF:16], ru, mi, "mi%d" % q, A.subtract)
+                scan(hs[:], "hs%d" % h, T.ha[:], "ha", bz[:], "bz%d" % h, A.mult, A.add, 0.3)
+                mm([(T[kt][:, 128 * k:128 * k + 128], hs[:, 128 * k:128 * k + 128], T.idb[:], True, True) for k in range(4)],
+                   ["hs%d" % h, "idb"], [kt], 0.35)
+                vts(T[kt][:], kt, T[kt][:], kt, T.ecol[:, 0:1], None, A.is_equal, None, 0.5, ["ecol"])
+                mm([(T[nt][0:8, 128 * k:128 * k + 128], bz[:, 128 * k:128 * k + 128:16], T.idb[:], True, True) for k in range(4)],
+                   ["bz%d" % h, "idb"], [nt], 0.35)
+                act(T[yn][:, HS[h]], "%s.%d" % (yn, h), T[nt][0:8, :], [nt], F.Copy, 0.57)
             ys.append(ylist(T[yn], halves(yn), 16384.0, -15360.0))
 
     store(T.yv[:], T[v][:], halves(v))
-    for d in range(N):
+
+    def yl_out(d, bank="nt"):
         s = (rank - d) % N
         z = zn[0] if d == 0 else (T["fr%d%d" % (TW - 1, d)][:], "fr%d%d" % (TW - 1, d))
-        letters(T.l0n[:, NC * s:NC * s + NC], "l0n", z[0], z[1], T.yl, s * K)
-    for t in range(TW):
+        letters(T.l0n[:, NC * s:NC * s + NC], "l0n", z[0], z[1], T.yl, s * K, bank)
+
+    def yi_out(t):
         letters(ys[t][0], ys[t][1], res[t][0], res[t][1], T.yi, t * K)
+    for f, a in ((yi_out, 1), (yi_out, 0), (yl_out, 0), (yl_out, 1), (yl_out, 2), (yi_out, 2)):
+        f(a)
+    yl_out(N - 1, "kt")
     emit(g, T, pl["tasks"])

from concourse.mybir import AluOpType as A, ActivationFunctionType as F

N, K, TW, W = 4, 1024, 3, 4608
HALF = K // 2
NC = K // 16
SH = 16
WIN = SH + 5120
PH = 2048
OFF = float(SH + PH)
FLAG = -16384.0
BYSCALAR = {(2, -2): (0, 1), (2, -1): (0, 1), (2, 0): (0, 1), (2, 1): (1,)}
SIGNV = ((TW - 1, N - 1),)
NU, NF, NB, NH = 40, 64, 64, 30

SCRATCH = {
    "jint": ("sbuf", [128, W], "int32"), "jw": ("sbuf", [128, WIN], "float32"),
    "cw": ("sbuf", [128, WIN], "bfloat16"), "cw3": ("sbuf", [128, WIN], "bfloat16"), "cst": ("sbuf", [128, 512], "bfloat16"),
    "ltn": ("sbuf", [8, N * K], "bfloat16"), "y0n": ("sbuf", [8, K], "bfloat16"),
    "sti": ("sbuf", [128, TW * NC], "int32"), "sta": ("sbuf", [128, TW * NC], "float32"),
    "stb": ("sbuf", [128, TW * NC], "float32"), "stu": ("sbuf", [128, TW * NC], "uint16"),
    "eb": ("sbuf", [128, 2048], "bfloat16"), "blk": ("sbuf", [128, 128], "bfloat16"),
    "idb": ("sbuf", [128, 128], "bfloat16"), "idn": ("sbuf", [128, 128], "bfloat16"), "idm": ("sbuf", [128, 128], "bfloat16"),
    "hx": ("sbuf", [128, 128], "bfloat16"), "gx": ("sbuf", [8, 2048], "bfloat16"), "bc8": ("sbuf", [8, 128], "bfloat16"),
    "pidx": ("sbuf", [128, 1], "int32"), "pxi": ("sbuf", [128, 1], "int32"), "xcol": ("sbuf", [128, 1], "float32"),
    "negx": ("sbuf", [128, 1], "float32"), "ecol": ("sbuf", [128, 1], "float32"),
    "jl0": ("sbuf", [128, NC], "float32"), "jl": ("sbuf", [128, NC], "float16"),
    "dl": ("sbuf", [128, HALF], "float32"), "ha": ("sbuf", [128, HALF], "bfloat16"),
    "lu": ("sbuf", [128, NC * NU], "uint16"), "lf": ("sbuf", [128, NC * NF], "float32"),
    "lb": ("sbuf", [128, NC * NB], "bfloat16"), "lh": ("sbuf", [128, NC * NH], "float16"),
    "l0n": ("sbuf", [128, NC * N], "bfloat16"), "zn0": ("sbuf", [128, NC * N], "bfloat16"), "absn": ("sbuf", [128, NC * N], "float32"),
    "mi": ("sbuf", [128, 32 * 4], "int32"),
    "js1": ("sbuf", [128, K], "float32"), "js2": ("sbuf", [128, K], "float32"),
}
BANKS = ("xa0", "xa1", "xc", "kt0", "kt1", "nt0", "nt1", "ms")
for _i in BANKS:
    SCRATCH[_i] = ("psum", [128, 512], "float32")
for _i in range(N):
    SCRATCH["mk%d" % _i] = ("sbuf", [128, K], "bfloat16")
for _i in range(3):
    SCRATCH["mt%d" % _i] = ("sbuf", [128, HALF], "bfloat16")
    SCRATCH["md%d" % _i] = ("sbuf", [128, K], "float16")
    for _n in ("v", "tm", "sg"):
        SCRATCH[_n + str(_i)] = ("sbuf", [128, K], "bfloat16")
for _i in range(7):
    SCRATCH["no%d" % _i] = ("sbuf", [8, K], "bfloat16")
for _i in range(2):
    SCRATCH["my%d" % _i] = ("sbuf", [128, K], "bfloat16")
    SCRATCH["yn%d" % _i] = ("sbuf", [8, K], "bfloat16")
    SCRATCH["gh%d" % _i] = ("sbuf", [128, HALF], "bfloat16")
    SCRATCH["run%d" % _i] = ("sbuf", [128, HALF], "float32")
    SCRATCH["bz%d" % _i] = ("sbuf", [128, HALF], "bfloat16")
    SCRATCH["hs%d" % _i] = ("sbuf", [128, HALF], "bfloat16")
SEMAPHORES = ["vq", "sq", "pq", "gq", "snt", "rcw"] + ["ld%d" % i for i in range(10)] + ["st%d" % i for i in range(8)]
for _d in range(1, N):
    SCRATCH["zi%d" % _d] = ("sbuf", [128, NC], "bfloat16")
    SEMAPHORES.append("rzi%d" % _d)
for _t in range(TW):
    SCRATCH["bh%d" % _t] = ("sbuf", [128, NC], "float16")
    SEMAPHORES.append("rh%d" % _t)
    for _d in range(1, N):
        _x = "%d%d" % (_t, _d)
        SCRATCH["br" + _x] = ("sbuf", [128, NC], "uint16")
        SCRATCH["fr" + _x] = ("sbuf", [128, NC], "bfloat16")
        SEMAPHORES += ["rb" + _x, "rf" + _x]
        if _d < N - 1:
            SCRATCH["cg" + _x] = ("sbuf", [128, 2 * (SH + HALF)], "bfloat16")
            SCRATCH["cs" + _x] = ("sbuf", [128, SH + K], "bfloat16")
            SEMAPHORES += ["rc%s0" % _x, "rc%s1" % _x]


def add(pl, eng, cost, reads, writes, fn, sem=None, lat=0.0, inc=None, after=None, kind="c"):
    tasks, last, rd = pl["tasks"], pl["last"], pl["rd"]
    i = len(tasks)
    deps = set(last[k] for k in list(reads) + list(writes) if k in last)
    for k in reads:
        if k in BANKS:
            deps |= set(j for j in rd.get(k, []) if tasks[j]["eng"] != eng)
    for k in writes:
        deps |= set(rd.get(k, []))
    for k in reads:
        rd.setdefault(k, []).append(i)
    for k in writes:
        last[k] = i
        rd[k] = []
    deps.discard(i)
    tdeps = deps if after is None else deps | set([after])
    tasks.append({"eng": eng, "cost": cost, "deps": sorted(deps), "tdeps": sorted(tdeps), "fn": fn, "sem": sem, "lat": lat,
                  "inc": inc, "kind": kind})
    return i


def order(tasks):
    n = len(tasks)
    succ = [[] for _ in range(n)]
    for i in range(n):
        for j in tasks[i]["tdeps"]:
            succ[j].append(i)
    pri = [0.0] * n
    own = [0.0] * n
    for i in range(n - 1, -1, -1):
        pri[i] = max([pri[j] for j in succ[i]] + [0.0]) + tasks[i]["cost"] + tasks[i]["lat"]
        own[i] = 1e6 - i if "first" in tasks[i] else pri[i]
    left = [len(tasks[i]["tdeps"]) for i in range(n)]
    rt = [0.0] * n
    todo = [i for i in range(n) if left[i] == 0]
    busy = {}
    start = [0.0] * n
    while todo:
        i = max(todo, key=lambda a: (own[a], -a))
        todo.remove(i)
        e, c = tasks[i]["eng"], tasks[i]["cost"]
        s = rt[i]
        if e != "R":
            b = busy.setdefault(e, [])
            k = 0
            while k < len(b) and b[k][1] <= s:
                k += 1
            while k < len(b) and b[k][0] < s + c:
                s = max(s, b[k][1])
                k += 1
            b.insert(k, (s, s + c))
        start[i] = s
        for j in succ[i]:
            left[j] -= 1
            rt[j] = max(rt[j], s + c + tasks[i]["lat"] + (0.03 if tasks[j]["eng"] == e else 0.08))
            if left[j] == 0:
                todo.append(j)
    return sorted(range(n), key=lambda a: (start[a], a))


def emit(g, T, tasks):
    seq = order(tasks)
    pos = dict((a, b) for b, a in enumerate(seq))
    q = {"V": g.vector, "S": g.scalar, "P": g.tensor, "G": g, "Y": g.sync}
    qsem = {"V": "vq", "S": "sq", "P": "pq", "G": "gq"}
    count = {}
    known = dict((e, {}) for e in q)
    tok = {}
    know = {}
    for i in seq:
        t = tasks[i]
        e = t["eng"]
        if e == "R":
            tok[i] = (t["sem"], t["inc"])
            know[i] = {t["sem"]: t["inc"]}
            continue
        kn = known[e]
        for j in sorted(t["deps"], key=lambda a: -pos[a]):
            s, v = tok[j]
            if kn.get(s, 0) >= v:
                continue
            q[e].wait_ge(T.sem[s], v)
            for s2 in know[j]:
                kn[s2] = max(kn.get(s2, 0), know[j][s2])
        ins = t["fn"]()
        if t["kind"] == "c":
            s = qsem[e]
            for x in ins:
                x.then_inc(T.sem[s], 1)
            count[s] = count.get(s, 0) + len(ins)
        elif t["kind"] == "d":
            s = t["sem"]
            ins[0].then_inc(T.sem[s], 16)
            count[s] = 16
        else:
            s = "snt"
            count[s] = count.get(s, 0) + t["inc"]
        tok[i] = (s, count[s])
        know[i] = dict(kn)
        know[i][s] = count[s]
    for s in count:
        if known["G"].get(s, 0) < count[s]:
            g.wait_ge(T.sem[s], count[s])


def rank_program(g, core, T, topo):
    rank = T.rank_of(core)
    if rank is None:
        return
    pl = {"tasks": [], "last": {}, "rd": {}}
    vec, sca, ten, syn = g.vector, g.scalar, g.tensor, g.sync
    cores = T.cores
    used = {}

    def take(kind):
        used[kind] = used.get(kind, -1) + 1
        return used[kind]

    def new(buf):
        n = take(buf)
        t = T[buf]
        return (t[:, NC * n:NC * n + NC], "%s.%d" % (buf, n), [t[:, NC * n + 32 * h:NC * n + 32 * h + 32] for h in range(2)])

    def rot(kind, n=3):
        return kind + str(take(kind) % n)

    def vts(out, ok, in0, ik, s1, s2, op0, op1, cost=0.08, more=()):
        args = (out, in0, s1, s2, op0) if op1 is None else (out, in0, s1, s2, op0, op1)
        return add(pl, "V", cost, [ik] + list(more), [ok], lambda: [vec.tensor_scalar(*args)])

    def vtt(out, ok, a, ak, b, bk, op, cost=0.08):
        return add(pl, "V", cost, [ak, bk], [ok], lambda: [vec.tensor_tensor(out, a, b, op)])

    def vcp(out, ok, a, ak, cost=0.08):
        return add(pl, "V", cost, [ak], [ok], lambda: [vec.tensor_copy(out, a)])

    def act(out, ok, in_, reads, func, cost, **kw):
        return add(pl, "S", cost, reads, [ok], lambda: [sca.activation(out, in_, func, **kw)])

    def scan(out, ok, d0, d0k, d1, d1k, op0, op1, cost):
        return add(pl, "V", cost, [d0k, d1k], [ok], lambda: [vec.tensor_tensor_scan(out, d0, d1, 0.0, op0, op1)])

    def mm(group, reads, writes, cost):
        return add(pl, "P", cost, reads, writes, lambda: [ten.matmul(*x) for x in group])

    def memset(ap, key, c, cost=0.08):
        return add(pl, "V", cost, [], [key], lambda: [vec.memset(ap, c)])

    def send(out, in_, sem, to, reads, key, lat, bulk=False):
        dst = cores[to]
        rid, pid, _ = topo.addr(dst)
        en = topo.engines(core, dst)
        en = en[1::2] if bulk else en[0::2]
        n = len(en)
        m = sum(1 << x for x in en)
        i = add(pl, "G", 0.4, reads, [], lambda: [g.remote_dma(out, in_, T.sem[sem], T.sem.snt, pid, rid, m)], inc=n, kind="r")
        return lambda: add(pl, "R", 0.0, [], key, None, sem=sem, inc=n, after=i, lat=lat)

    def load(eng, out, in_, key, lat):
        qq = syn if eng == "Y" else sca
        i = add(pl, eng, 0.1, [], [key], lambda: [qq.dma_start(out, in_)], sem="ld%d" % take("ld"), lat=lat, kind="d")
        pl["tasks"][i]["first"] = True

    def store(out, in_, reads):
        add(pl, "Y", 0.1, reads, [], lambda: [syn.dma_start(out, in_)], sem="st%d" % take("st"), lat=2.0, kind="d")

    def halves(k):
        return [k + ".0", k + ".1"]

    HS = [slice(0, HALF), slice(HALF, K)]

    load("S", T.y0n[:], T.y0[:], "y0n", 3.0)
    load("S", T.sti[:], T.st[:], "sti", 3.2)
    load("S", T.ltn[:], T.lt[:], "ltn", 5.0)
    at = 2.0
    for p in range(5):
        a, b = 1024 * p, min(W, 1024 * p + 1024)
        at += (b - a) * 512 / 2.2e5
        load("Y", T.jint[:, a:b], T.jm[:, a:b], "jint%d" % p, at)
    load("Y", T.cst[:], T.cf[:, 4096:W], "cst", at + 0.9)
    load("Y", T.cw[:, SH:SH + 4096], T.cf[:, 0:4096], "cwa", at + 5.4)

    def gsel(ap, key, pat, op, base, cm, cost=0.42, after=None):
        return add(pl, "G", cost, [key], [key], lambda: [g.affine_select(ap, ap, pat, op, 0.0, base, cm)], after=after)
    memset(T.idb[:], "idb", 1.0, 0.15)
    memset(T.blk[:], "blk", 1.0, 0.15)
    memset(T.bc8[:], "bc8", 1.0, 0.15)
    memset(T.eb[:], "eb", 0.0, 0.9)
    memset(T.gx[:], "gx", 1.0, 0.9)
    memset(T.hx[:], "hx", -1.0 / 1024.0, 0.15)
    add(pl, "G", 0.14, [], ["pidx"], lambda: [g.iota(T.pidx[:], [[1, 1]], 0, 1)])
    gsel(T.blk[:], "blk", [[-16, 8], [0, 16]], A.is_ge, 0, 1)
    i = gsel(T.blk[:], "blk", [[16, 8], [0, 16]], A.is_ge, 15, -1)
    gsel(T.bc8[:], "bc8", [[-1, 8], [0, 16]], A.is_equal, 0, 1)
    i = gsel(T.idb[:], "idb", [[-1, 128]], A.is_equal, 0, 1, 0.42, i)
    add(pl, "G", 0.25, [], ["jl0"], lambda: [g.iota(T.jl0[:], [[0, 2], [16, NC // 2]], -PH, 0, allow_small_or_imprecise_dtypes=True)])
    gsel(T.hx[:], "hx", [[-1, 16], [-16, 8]], A.is_equal, 0, 1, 0.42, i)
    gsel(T.gx[:], "gx", [[1, 16], [-16, 8], [-1, 16]], A.is_equal, 0, 16, 3.6, i)

    add(pl, "V", 0.06, ["pidx"], ["pxi"], lambda: [vec.tensor_scalar(T.pxi[:], T.pidx[:], 15, None, A.bitwise_and)])
    vcp(T.xcol[:], "xcol", T.pxi[:], "pxi")
    vts(T.negx[:], "negx", T.xcol[:], "xcol", -1.0, None, A.mult, None)
    vts(T.ecol[:], "ecol", T.xcol[:], "xcol", -1.0 / 16.0, 15.0 / 16.0, A.mult, A.add)
    vts(T.jl[:], "jl", T.jl0[:], "jl0", T.xcol[:, 0:1], None, A.add, None, more=["xcol"])
    add(pl, "S", 1.3, ["blk"], ["eb"],
        lambda: [sca.activation(T.eb[:, 128 * x + x:128 * x + 128:16], T.blk[:, x:128:16], F.Copy) for x in range(16)])
    vts(T.idn[:], "idn", T.idb[:], "idb", -1.0, None, A.mult, None, 0.12)
    vts(T.idm[:], "idm", T.idb[:], "idb", -0.5, None, A.mult, None, 0.12)
    memset(T.dl[:], "dl", 1.0 / 16.0, 0.45)
    memset(T.dl[:, 0:HALF:16], "dl", -1000.0)
    memset(T.ha[:], "ha", 1.0, 0.3)
    memset(T.ha[:, 0:HALF:16], "ha", 0.0)
    memset(T.bz0[:], "bz0", 0.0, 0.3)
    memset(T.bz1[:], "bz1", 0.0, 0.3)
    memset(T.jw[:, 0:SH], "jwz", 0.0)
    memset(T.jw[:, SH + 4096:WIN], "jwu", 0.0, 0.9)
    memset(T.cw[:, 0:SH], "cwz", 0.0)
    memset(T.cw[:, SH + 4096:WIN], "cwu", 0.0, 0.5)
    for t in range(TW):
        for d in range(1, N - 1):
            x = "%d%d" % (t, d)
            memset(T["cg" + x][:, 0:SH], "cgz" + x, 0.0)
            memset(T["cs" + x][:, HALF:HALF + SH], "csz" + x, 0.0)

    for h in range(2):
        nt = "nt%d" % h
        mm([(T[nt][:, 0:HALF], T.bc8[:], T.y0n[:, HS[h]], True, True)], ["bc8", "y0n"], [nt], 0.35)
        vts(T.my0[:, HS[h]], "my0.%d" % h, T[nt][:, 0:HALF], nt, T.xcol[:, 0:1], None, A.is_equal, None, 0.5, ["xcol"])
    mm([(T.ms[:, 0:256], T.gx[:, 128 * r:128 * r + 128], T.ltn[:, r:N * K:16], r == 0, r == 15) for r in range(16)],
       ["gx", "ltn"], ["ms"], 2.5)
    vts(T.zn0[:], "zn0", T.ms[:, 0:256], "ms", 15.5, FLAG, A.is_ge, A.mult, 0.25)
    vts(T.absn[:], "absn", T.ms[:, 0:256], "ms", 15.5, None, A.is_ge, None, 0.25)
    vts(T.l0n[:], "l0n", T.ms[:, 0:256], "ms", -1024.0, None, A.mult, None, 0.25)
    for d in range(N):
        for h in range(2):
            bk = ("xa0", "xa1", "xc")[take("mb") % 3]
            mt = rot("mt")
            c = ((rank - d) % N) * K + HALF * h
            mm([(T[bk][:, 0:HALF], T.bc8[:], T.ltn[:, c:c + HALF], True, True)], ["bc8", "ltn"], [bk], 0.35)
            act(T[mt][:], mt, T[bk][:, 0:HALF], [bk, "negx"], F.Abs, 0.5, bias=T.negx[:, 0:1])
            act(T["mk%d" % d][:, HS[h]], "mk%d.%d" % (d, h), T[mt][:], [mt], F.Relu, 0.5, bias=1.0, scale=-1.0)
    for d in range(1, N):
        s = (rank - d) % N
        send(T["zi%d" % d][:], T.zn0[:, NC * s:NC * s + NC], "rzi%d" % d, s, ["zn0"], ["zi%d" % d], 2.0)()

    vts(T.sta[:], "sta", T.sti[:], "sti", 2.0, -4096.0, A.mult, A.add, 0.2)
    vtt(T.stb[:], "stb", T.sti[:], "sti", T.sta[:], "sta", A.max, 0.35)
    vts(T.stu[:], "stu", T.stb[:], "stb", float(SH), None, A.add, None, 0.2)
    for p in range(9):
        bk = "kt%d" % (p % 2)
        a = 512 * p
        src, ik = T.jint[:, a:a + 512], "jint%d" % (p // 2)
        vts(T[bk][:], bk, src, ik, 4096.0, -6144.0, A.max, A.add, 0.48)
        out, ok = (T.jw[:, SH + a:SH + a + 512], "jw%d" % p) if p < 8 else (T.jw[:, SH + 4096:WIN:2], "jwu")
        vtt(out, ok, src, ik, T[bk][:], bk, A.add, 0.48)
    JW = ["jwz", "jwu"] + ["jw%d" % p for p in range(8)]
    act(T.cw[:, SH + 4096:WIN:2], "cwu", T.cst[:], ["cst"], F.Copy, 0.48)
    CW = ["cwz", "cwu", "cwa"]
    send(T.cw3[:], T.cw[:], "rcw", (rank + 1) % N, CW, ["cw3"], 9.0, True)()

    def summed(md, keep=None):
        bk = rot("xa", 2)
        x = T[bk][:, 0:NC]
        grp = [(x, T.eb[:, 128 * r:128 * r + 128], T[md][:, r:K:16], r == 0, r == 15 and keep is None) for r in range(16)]
        if keep is not None:
            grp.append((x, T.idb[:], keep[0], False, True))
        mm(grp, ["eb", "idb"] + halves(md) + ([keep[1]] if keep is not None else []), [bk], 0.65)
        return x, bk

    def image(lst, lk, mask, mkeys, keep=None):
        md = rot("md")
        add(pl, "V", 1.65, JW + [lk] + mkeys, halves(md), lambda: [vec.tensor_tensor(T[md][:], T.jw[:].indirect(lst), mask[:], A.mult)])
        return summed(md, keep)

    for t in range(1, TW):
        for h in range(2):
            c = NC * t + 32 * h
            act(T["js%d" % t][:, HS[h]], "js%d.%d" % (t, h), T.jw[:].indirect(T.stu[:, c:c + 32]), JW + ["stu"], F.Identity, 0.86)

    def start(t):
        if t == 0:
            return image(T.stu[:, 0:NC], "stu", T.my0, halves("my0"))
        md = rot("md")
        for h in range(2):
            kt = "kt%d" % h
            vtt(T[md][:, HS[h]], "%s.%d" % (md, h), T["js%d" % t][:, HS[h]], "js%d.%d" % (t, h), T[kt][:], kt, A.mult, 0.53)
        x = summed(md)
        if t < TW - 1:
            for h in range(2):
                act(T["my%d" % t][:, HS[h]], "my%d.%d" % (t, h), T["kt%d" % h][:], ["kt%d" % h], F.Copy, 0.57)
        return x

    def tolist(x, xk):
        l = new("lu")
        vts(l[0], l[1], x, xk, OFF, 0.0, A.add, A.max)
        return l

    def bslot(lst, lk, mask, mkeys, absent, present, prev, want, wantl):
        if prev is None:
            prev = new("lf")
            vts(prev[0], prev[1], lst, lk, -OFF, None, A.add, None)
        if present is None:
            k = new("lh")
            vtt(k[0], k[1], prev[0], prev[1], absent[0], absent[1], A.mult)
            x = image(lst, lk, mask, mkeys, k)
            l = tolist(x[0], x[1]) if wantl else None
            b = None
            if want:
                b = new("lh")
                vcp(b[0], b[1], x[0], x[1])
            return b, l
        k, a, b = new("lf"), new("lf"), new("lh")
        vtt(k[0], k[1], prev[0], prev[1], absent[0], absent[1], A.mult)
        x = image(lst, lk, mask, mkeys)
        vtt(a[0], a[1], x[0], x[1], present[0], present[1], A.mult)
        vtt(b[0], b[1], a[0], a[1], k[0], k[1], A.add)
        return b, tolist(b[0], b[1]) if wantl else None

    def flags(z, zk):
        n, p = new("lf"), new("lf")
        act(n[0], n[1], z, [zk], F.Copy, 0.15, scale=1.0 / FLAG)
        act(p[0], p[1], z, [zk], F.Identity, 0.15, bias=1.0, scale=-1.0 / FLAG)
        return n, p

    def gather_c(out, okeys, l):
        for h in range(2):
            act(out[h], okeys[h], T.cw[:].indirect(l[2][h]), CW + [l[1]], F.Identity, 0.86)

    def vslot(v, base, zn, dead, wins, wkeys, at):
        u = T.xc[:, NC:2 * NC]
        grp = [(u, T.idb[:], base[0], True, False), (u, T.idb[:], zn[0], False, dead is None)]
        dk = [] if dead is None else [dead[1]]
        if dead is not None:
            grp.append((u, T.idb[:], dead[0], False, True))
        mm(grp, ["idb", base[1], zn[1]] + dk, ["xc"], 0.1)
        l = tolist(u, "xc")
        tm, nv = rot("tm"), rot("v")
        sg = "sg" + tm[2:]
        for h in range(2):
            c = HS[h]
            vk, tk, sk, nk = ["%s.%d" % (x, h) for x in (v, tm, sg, nv)]
            vi, src, srk, cl = T[v][:, c], T[tm][:, c], tk, 0.28
            if h in BYSCALAR.get(at, ()):
                gh = rot("gh", 2)
                act(T[gh][:], gh, wins[h].indirect(l[2][h]), wkeys(h) + [l[1]], F.Identity, 0.85)
                src, srk, cl = T["kt%d" % h][:], "kt%d" % h, 0.55
                mm([(src, T.idb[:], vi, True, False), (src, T.idb[:], T[gh][:], False, True)], ["idb", vk, gh], [srk], 0.5)
            else:
                add(pl, "V", 0.83, wkeys(h) + [l[1], vk], [tk],
                    lambda src=src, h=h, vi=vi: [vec.tensor_tensor(src, wins[h].indirect(l[2][h]), vi, A.add)])
            if h and at in SIGNV:
                vts(T[sg][:, c], sk, src, srk, 0.0, 0.5, A.is_ge, A.subtract, 0.28)
            else:
                act(T[sg][:, c], sk, src, [srk], F.Sign, 0.57, bias=0.5)
            vts(T[nv][:, c], nk, src, srk, 255.0, -255.0, A.min, A.max, cl)
        o = T.xc[:, 0:NC]
        grp = [(o, T.idm[:], zn[0], True, False)]
        if dead is not None:
            grp.append((o, T.idb[:], dead[0], False, False))
        grp += [(o, T.eb[:, 128 * r:128 * r + 128], T[sg][:, r:K:16], False, r == 15) for r in range(16)]
        mm(grp, ["idm", "idb", zn[1], "eb"] + halves(sg) + dk, ["xc"], 0.7)
        nd, nz = new("lb"), new("lb")
        vts(nd[0], nd[1], o, "xc", -0.25, FLAG, A.is_le, A.mult)
        if dead is None:
            vtt(nz[0], nz[1], zn[0], zn[1], nd[0], nd[1], A.add)
        elif at == (TW - 1, N - 1):
            zd = new("lb")
            vtt(zd[0], zd[1], zn[0], zn[1], dead[0], dead[1], A.subtract)
            vtt(nz[0], nz[1], zd[0], zd[1], nd[0], nd[1], A.add)
        else:
            q = T.ms[:, 0:NC]
            mm([(q, T.idb[:], zn[0], True, False), (q, T.idn[:], dead[0], False, False), (q, T.idb[:], nd[0], False, True)],
               ["idb", "idn", zn[1], dead[1], nd[1]], ["ms"], 0.1)
            act(nz[0], nz[1], q, ["ms"], F.Copy, 0.15)
        return nv, nd, nz

    def ylist(rows, keys, a, b):
        l = new("lb")
        mm([(T.ms[:, 0:NC], T.gx[:, 128 * r:128 * r + 128], rows[:, r:K:16], r == 0, r == 15) for r in range(16)],
           ["gx"] + keys, ["ms"], 0.7)
        vts(l[0], l[1], T.ms[:, 0:NC], "ms", a, b, A.mult, A.add)
        return l

    def letters(y, yk, z, zk, out, oc, bank="nt"):
        f = new("lb")
        vtt(f[0], f[1], y, yk, z, zk, A.min)
        no = rot("no", 7)
        for h in range(2):
            nt = bank + str(h)
            mm([(T[nt][0:8, r:512:16], T.hx[:, 8 * r:8 * r + 8], f[2][h], True, True) for r in range(16)], ["hx", f[1]], [nt], 0.4)
            if h:
                vcp(T[no][:, HS[h]], no + ".1", T[nt][0:8, :], nt, 0.55)
            else:
                act(T[no][:, HS[h]], no + ".0", T[nt][0:8, :], [nt], F.Copy, 0.57)
        store(out[:, oc:oc + K], T[no][:], halves(no))

    zn = [(T.zn0[:, NC * rank:NC * rank + NC], "zn0")] + [(T["zi%d" % d][:], "zi%d" % d) for d in range(1, N)]
    res = []
    ys = [ylist(T.y0n, ["y0n"], -1024.0, 0.0)]
    for t in range(TW):
        x = start(t)
        l = lstart = tolist(x[0], x[1])
        todo = [(T["my%d" % i], halves("my%d" % i), res[i]) for i in range(t - 1, -1, -1)] + [(T.mk0, halves("mk0"), zn[0])]
        chain = []
        prev = None
        for mask, mkeys, z in todo:
            n, p = flags(z[0], z[1]) if t else ((T.absn[:, NC * rank:NC * rank + NC], "absn"), None)
            prev, l = bslot(l[0], l[1], mask, mkeys, n, p, prev, True, True)
            chain.append(prev)
        arrive = send(T["br%d1" % t][:], l[0], "rb%d1" % t, (rank + 1) % N, [l[1]], ["br%d1" % t], 1.9)
        v = rot("v")
        gather_c([T[v][:, HS[0]], T[v][:, HS[1]]], halves(v), lstart)
        dead = None
        for j in range(len(todo)):
            v, dead, nz = vslot(v, chain[j], todo[j][2], dead, [T.cw[:], T.cw[:]], lambda h: CW, (t, -j))
            if j < t:
                res[t - 1 - j] = nz
            else:
                zn[0] = nz
        pend = []
        for d in range(1, N):
            x = "%d%d" % (t, d)
            arrive()
            home = (rank - d) % N
            n, p = flags(T["fr%d%d" % (t - 1, d)][:], "fr%d%d" % (t - 1, d)) if t else ((T.absn[:, NC * home:NC * home + NC], "absn"), None)
            lastd = d == N - 1
            b, l = bslot(T["br" + x][:], "br" + x, T["mk%d" % d], halves("mk%d" % d), n, p, None, lastd, not lastd)
            if lastd:
                pend.append(send(T["bh%d" % t][:], b[0], "rh%d" % t, home, [b[1]], ["bh%d" % t], 1.9))
                continue
            k = "%d%d" % (t, d + 1)
            arrive = send(T["br" + k][:], l[0], "rb" + k, (rank + 1) % N, [l[1]], ["br" + k], 1.9)
            cs, cg, ck, ak = T["cs" + x], T["cg" + x], halves("cs" + x), halves("cg" + x)
            gather_c([cs[:, 0:HALF], cs[:, SH + HALF:SH + K]], ck, l)
            if d == N - 2:
                pend.append(send(cg[:, SH:SH + HALF], cs[:, 0:HALF], "rc%s0" % x, home, ck[:1], ak[:1], 2.6, True))
                pend.append(send(cg[:, SH + HALF:2 * (SH + HALF)], cs[:, HALF:SH + K], "rc%s1" % x, home, [ck[1], "csz" + x], ak[1:], 2.6, True))
            else:
                pend.append(send(cg[:, SH:2 * (SH + HALF)], cs[:], "rc%s0" % x, home, ck + ["csz" + x], ak, 3.0, True))
        for f in pend:
            f()
        for d in range(1, N):
            x = "%d%d" % (t, d)
            if d == N - 1:
                v, dead, nz = vslot(v, (T["bh%d" % t][:], "bh%d" % t), zn[d], dead, [T.cw3[:], T.cw3[:]], lambda h: ["cw3"], (t, d))
            else:
                cg = T["cg" + x]
                v, dead, nz = vslot(v, (T.jl[:], "jl"), zn[d], dead, [cg[:, 0:SH + HALF], cg[:, SH + HALF:2 * (SH + HALF)]],
                                    lambda h, x=x: ["cgz" + x if h == 0 else "cg%s.1" % x, "cg%s.%d" % (x, h)], (t, d))
            zn[d] = nz
            send(T["fr" + x][:], nz[0], "rf" + x, (rank + d) % N, [nz[1]], ["fr" + x], 2.0)()
        res.append(dead)
        if t < TW - 1:
            yn = "yn%d" % t
            for h in range(2):
                kt, nt, ru = "kt%d" % h, "nt%d" % h, "run%d" % h
                c0 = HALF * h
                mm([(T[kt][:, 128 * k:128 * k + 128], T[v][:, c0 + 128 * k:c0 + 128 * k + 128], T.idb[:], True, True) for k in range(4)],
                   ["%s.%d" % (v, h), "idb"], [kt], 0.35)
                scan(T[ru][:], ru, T.dl[:], "dl", T[kt][:], kt, A.add, A.max, 0.5)
                q = 2 * t + h
                mi, bz, hs = T.mi[:, 32 * q:32 * q + 32], T["bz%d" % h], T["hs%d" % h]
                vts(mi, "mi%d" % q, T[ru][:, 15:HALF:16], ru, -15.0 / 32.0, None, A.add, None)
                vtt(bz[:, 0:HALF:16], "bz%d" % h, T[ru][:, 15:HALF:16], ru, mi, "mi%d" % q, A.subtract)
                scan(hs[:], "hs%d" % h, T.ha[:], "ha", bz[:], "bz%d" % h, A.mult, A.add, 0.3)
                mm([(T[kt][:, 128 * k:128 * k + 128], hs[:, 128 * k:128 * k + 128], T.idb[:], True, True) for k in range(4)],
                   ["hs%d" % h, "idb"], [kt], 0.35)
                vts(T[kt][:], kt, T[kt][:], kt, T.ecol[:, 0:1], None, A.is_equal, None, 0.5, ["ecol"])
                mm([(T[nt][0:8, 128 * k:128 * k + 128], bz[:, 128 * k:128 * k + 128:16], T.idb[:], True, True) for k in range(4)],
                   ["bz%d" % h, "idb"], [nt], 0.35)
                act(T[yn][:, HS[h]], "%s.%d" % (yn, h), T[nt][0:8, :], [nt], F.Copy, 0.57)
            ys.append(ylist(T[yn], halves(yn), 16384.0, -15360.0))

    store(T.yv[:], T[v][:], halves(v))

    def yl_out(d, bank="nt"):
        s = (rank - d) % N
        z = zn[0] if d == 0 else (T["fr%d%d" % (TW - 1, d)][:], "fr%d%d" % (TW - 1, d))
        letters(T.l0n[:, NC * s:NC * s + NC], "l0n", z[0], z[1], T.yl, s * K, bank)

    def yi_out(t):
        letters(ys[t][0], ys[t][1], res[t][0], res[t][1], T.yi, t * K)
    for f, a in ((yi_out, 1), (yi_out, 0), (yl_out, 0), (yl_out, 1), (yl_out, 2), (yi_out, 2)):
        f(a)
    yl_out(N - 1, "kt")
    emit(g, T, pl["tasks"])
